import numpy as np
import ml_dtypes

BF16 = ml_dtypes.bfloat16


def bf(x):
    return np.asarray(x, np.float32).astype(BF16)


def f32(x):
    return np.asarray(x, np.float32)


def f64(x):
    return np.asarray(x).astype(np.float64)


def striped(idx):
    return np.tile(idx.reshape(-1, 16).T, (8, 1))


S, K, M, N, E, Q, H = 256, 128, 512, 512, 4, 128, 256


def sigmoid(v):
    return 1.0 / (1.0 + np.exp(-v))


def two_experts():
    first = np.random.permutation(S).reshape(E, S // E)
    return np.concatenate([np.random.permutation(np.concatenate([first[e], first[(e + 1) % E]])) for e in range(E)])


def setup_inputs():
    return {"table": bf(np.random.standard_normal((K, S))), "w": bf(np.random.standard_normal((E, K, M)) / np.sqrt(K)), "offs": striped(two_experts())}


def reference(table, w, offs):
    idx = offs[:16].T.reshape(-1)
    x = f64(table)[:, idx]
    y = np.concatenate([f64(w)[e].T @ x[:, e * Q : (e + 1) * Q] for e in range(E)], axis=1)
    return y[:H] * sigmoid(y[H:])

@@ -1,0 +1,49 @@
+import concourse.mybir as mybir
+
+BF16, F32, U16 = mybir.dt.bfloat16, mybir.dt.float32, mybir.dt.uint16
+SIGMOID = mybir.ActivationFunctionType.Sigmoid
+MULT = mybir.AluOpType.mult
+
+P = 128
+TOKENS = 256
+EXPERTS = 4
+PIECE = 128
+M = 512
+HALF_BLOCKS = 2
+PIECE_COLUMNS = PIECE // 16
+
+FLOPS = 2 * P * M * EXPERTS * PIECE
+
+
+def tile_gather_matmul_kernel(tc, table, w, offs, out):
+    nc = tc.nc
+    out_blocks = out.rearrange("(b p) j -> p b j", p=P)
+    with (
+        tc.tile_pool(name="held", bufs=1) as held,
+        tc.psum_pool(name="psum", bufs=1) as psum,
+    ):
+        offsets = held.tile([P, EXPERTS * PIECE_COLUMNS], U16, name="offsets")
+        nc.sync.dma_start(offsets[:], offs)
+        tokens = held.tile([P, TOKENS], BF16, name="tokens")
+        nc.scalar.dma_start(tokens[:], table)
+        weights = [held.tile([P, M], BF16, name=f"weights{e}") for e in range(EXPERTS)]
+        for e in range(EXPERTS):
+            queue = nc.sync if e % 2 == 0 else nc.scalar
+            queue.dma_start(weights[e][:], w[e])
+
+        for e in range(EXPERTS):
+            picked = tokens[:].indirect(offsets[:, e * PIECE_COLUMNS : (e + 1) * PIECE_COLUMNS])
+            gates = psum.tile([P, HALF_BLOCKS, PIECE], F32, name=f"gates{e}")
+            values = psum.tile([P, HALF_BLOCKS, PIECE], F32, name=f"values{e}")
+            for b in range(HALF_BLOCKS):
+                first = (HALF_BLOCKS + b) * P
+                nc.tensor.matmul(gates[:, b, :], weights[e][:, first : first + P], picked, start=True, stop=True)
+            for b in range(HALF_BLOCKS):
+                first = b * P
+                nc.tensor.matmul(values[:, b, :], weights[e][:, first : first + P], picked, start=True, stop=True)
+
+            opened = held.tile([P, HALF_BLOCKS, PIECE], F32, name=f"opened{e}")
+            nc.scalar.activation(opened[:], gates[:], SIGMOID)
+            gated = held.tile([P, HALF_BLOCKS, PIECE], F32, name=f"gated{e}")
+            nc.vector.tensor_tensor(gated[:], values[:], opened[:], MULT)
+            nc.sync.dma_start(out_blocks[:, :, e * PIECE : (e + 1) * PIECE], gated[:])

@@ -9,6 +9,7 @@ TOKENS = 256
 EXPERTS = 4
 PIECE = 128
 M = 512
+HALF = M // 2
 HALF_BLOCKS = 2
 PIECE_COLUMNS = PIECE // 16
 
@@ -26,21 +27,20 @@ def tile_gather_matmul_kernel(tc, table, w, offs, out):
         nc.sync.dma_start(offsets[:], offs)
         tokens = held.tile([P, TOKENS], BF16, name="tokens")
         nc.scalar.dma_start(tokens[:], table)
-        weights = [held.tile([P, M], BF16, name=f"weights{e}") for e in range(EXPERTS)]
+        gate_weights = [held.tile([P, HALF], BF16, name=f"gate_weights{e}") for e in range(EXPERTS)]
+        value_weights = [held.tile([P, HALF], BF16, name=f"value_weights{e}") for e in range(EXPERTS)]
         for e in range(EXPERTS):
-            queue = nc.sync if e % 2 == 0 else nc.scalar
-            queue.dma_start(weights[e][:], w[e])
+            nc.sync.dma_start(gate_weights[e][:], w[e, :, HALF:M])
+            nc.scalar.dma_start(value_weights[e][:], w[e, :, 0:HALF])
 
         for e in range(EXPERTS):
             picked = tokens[:].indirect(offsets[:, e * PIECE_COLUMNS : (e + 1) * PIECE_COLUMNS])
             gates = psum.tile([P, HALF_BLOCKS, PIECE], F32, name=f"gates{e}")
             values = psum.tile([P, HALF_BLOCKS, PIECE], F32, name=f"values{e}")
             for b in range(HALF_BLOCKS):
-                first = (HALF_BLOCKS + b) * P
-                nc.tensor.matmul(gates[:, b, :], weights[e][:, first : first + P], picked, start=True, stop=True)
+                nc.tensor.matmul(gates[:, b, :], gate_weights[e][:, b * P : (b + 1) * P], picked, start=True, stop=True)
             for b in range(HALF_BLOCKS):
-                first = b * P
-                nc.tensor.matmul(values[:, b, :], weights[e][:, first : first + P], picked, start=True, stop=True)
+                nc.tensor.matmul(values[:, b, :], value_weights[e][:, b * P : (b + 1) * P], picked, start=True, stop=True)
 
             opened = held.tile([P, HALF_BLOCKS, PIECE], F32, name=f"opened{e}")
             nc.scalar.activation(opened[:], gates[:], SIGMOID)

@@ -12,6 +12,7 @@ M = 512
 HALF = M // 2
 HALF_BLOCKS = 2
 PIECE_COLUMNS = PIECE // 16
+HALVED_EXPERTS = 2
 
 FLOPS = 2 * P * M * EXPERTS * PIECE
 
@@ -27,11 +28,22 @@ def tile_gather_matmul_kernel(tc, table, w, offs, out):
         nc.sync.dma_start(offsets[:], offs)
         tokens = held.tile([P, TOKENS], BF16, name="tokens")
         nc.scalar.dma_start(tokens[:], table)
-        gate_weights = [held.tile([P, HALF], BF16, name=f"gate_weights{e}") for e in range(EXPERTS)]
-        value_weights = [held.tile([P, HALF], BF16, name=f"value_weights{e}") for e in range(EXPERTS)]
+        gate_weights = []
+        value_weights = []
         for e in range(EXPERTS):
-            nc.sync.dma_start(gate_weights[e][:], w[e, :, HALF:M])
-            nc.scalar.dma_start(value_weights[e][:], w[e, :, 0:HALF])
+            if e < HALVED_EXPERTS:
+                gate_half = held.tile([P, HALF], BF16, name=f"gate_half{e}")
+                nc.sync.dma_start(gate_half[:], w[e, :, HALF:M])
+                value_half = held.tile([P, HALF], BF16, name=f"value_half{e}")
+                nc.scalar.dma_start(value_half[:], w[e, :, 0:HALF])
+                gate_weights.append(gate_half[:])
+                value_weights.append(value_half[:])
+            else:
+                whole = held.tile([P, M], BF16, name=f"whole{e}")
+                queue = nc.sync if e % 2 == 0 else nc.scalar
+                queue.dma_start(whole[:], w[e])
+                gate_weights.append(whole[:, HALF:M])
+                value_weights.append(whole[:, 0:HALF])
 
         for e in range(EXPERTS):
             picked = tokens[:].indirect(offsets[:, e * PIECE_COLUMNS : (e + 1) * PIECE_COLUMNS])

@@ -13,6 +13,7 @@ HALF = M // 2
 HALF_BLOCKS = 2
 PIECE_COLUMNS = PIECE // 16
 HALVED_EXPERTS = 2
+PSUM_BANKS = 8
 
 FLOPS = 2 * P * M * EXPERTS * PIECE
 
@@ -22,7 +23,7 @@ def tile_gather_matmul_kernel(tc, table, w, offs, out):
     out_blocks = out.rearrange("(b p) j -> p b j", p=P)
     with (
         tc.tile_pool(name="held", bufs=1) as held,
-        tc.psum_pool(name="psum", bufs=1) as psum,
+        tc.psum_pool(name="psum", bufs=PSUM_BANKS) as psum,
     ):
         offsets = held.tile([P, EXPERTS * PIECE_COLUMNS], U16, name="offsets")
         nc.sync.dma_start(offsets[:], offs)
@@ -47,15 +48,22 @@ def tile_gather_matmul_kernel(tc, table, w, offs, out):
 
         for e in range(EXPERTS):
             picked = tokens[:].indirect(offsets[:, e * PIECE_COLUMNS : (e + 1) * PIECE_COLUMNS])
-            gates = psum.tile([P, HALF_BLOCKS, PIECE], F32, name=f"gates{e}")
-            values = psum.tile([P, HALF_BLOCKS, PIECE], F32, name=f"values{e}")
+            steps = HALF_BLOCKS if e == EXPERTS - 1 else 1
+            blocks = HALF_BLOCKS // steps
+            gates = [psum.tile([P, blocks, PIECE], F32, name=f"gates{e}_{s}", tag="bank") for s in range(steps)]
+            values = [psum.tile([P, blocks, PIECE], F32, name=f"values{e}_{s}", tag="bank") for s in range(steps)]
             for b in range(HALF_BLOCKS):
-                nc.tensor.matmul(gates[:, b, :], gate_weights[e][:, b * P : (b + 1) * P], picked, start=True, stop=True)
+                nc.tensor.matmul(
+                    gates[b // blocks][:, b % blocks, :], gate_weights[e][:, b * P : (b + 1) * P], picked, start=True, stop=True
+                )
             for b in range(HALF_BLOCKS):
-                nc.tensor.matmul(values[:, b, :], value_weights[e][:, b * P : (b + 1) * P], picked, start=True, stop=True)
+                nc.tensor.matmul(
+                    values[b // blocks][:, b % blocks, :], value_weights[e][:, b * P : (b + 1) * P], picked, start=True, stop=True
+                )
 
-            opened = held.tile([P, HALF_BLOCKS, PIECE], F32, name=f"opened{e}")
-            nc.scalar.activation(opened[:], gates[:], SIGMOID)
-            gated = held.tile([P, HALF_BLOCKS, PIECE], F32, name=f"gated{e}")
-            nc.vector.tensor_tensor(gated[:], values[:], opened[:], MULT)
-            nc.sync.dma_start(out_blocks[:, :, e * PIECE : (e + 1) * PIECE], gated[:])
+            for s in range(steps):
+                opened = held.tile([P, blocks, PIECE], F32, name=f"opened{e}_{s}")
+                nc.scalar.activation(opened[:], gates[s][:], SIGMOID)
+                gated = held.tile([P, blocks, PIECE], F32, name=f"gated{e}_{s}")
+                nc.vector.tensor_tensor(gated[:], values[s][:], opened[:], MULT)
+                nc.sync.dma_start(out_blocks[:, s * blocks : (s + 1) * blocks, e * PIECE : (e + 1) * PIECE], gated[:])

@@ -14,6 +14,7 @@ HALF_BLOCKS = 2
 PIECE_COLUMNS = PIECE // 16
 HALVED_EXPERTS = 2
 PSUM_BANKS = 8
+DMA_ALIGN = 256
 
 FLOPS = 2 * P * M * EXPERTS * PIECE
 
@@ -27,20 +28,20 @@ def tile_gather_matmul_kernel(tc, table, w, offs, out):
     ):
         offsets = held.tile([P, EXPERTS * PIECE_COLUMNS], U16, name="offsets")
         nc.sync.dma_start(offsets[:], offs)
-        tokens = held.tile([P, TOKENS], BF16, name="tokens")
+        tokens = held.tile([P, TOKENS], BF16, name="tokens", align_bytes=DMA_ALIGN)
         nc.scalar.dma_start(tokens[:], table)
         gate_weights = []
         value_weights = []
         for e in range(EXPERTS):
             if e < HALVED_EXPERTS:
-                gate_half = held.tile([P, HALF], BF16, name=f"gate_half{e}")
+                gate_half = held.tile([P, HALF], BF16, name=f"gate_half{e}", align_bytes=DMA_ALIGN)
                 nc.sync.dma_start(gate_half[:], w[e, :, HALF:M])
-                value_half = held.tile([P, HALF], BF16, name=f"value_half{e}")
+                value_half = held.tile([P, HALF], BF16, name=f"value_half{e}", align_bytes=DMA_ALIGN)
                 nc.scalar.dma_start(value_half[:], w[e, :, 0:HALF])
                 gate_weights.append(gate_half[:])
                 value_weights.append(value_half[:])
             else:
-                whole = held.tile([P, M], BF16, name=f"whole{e}")
+                whole = held.tile([P, M], BF16, name=f"whole{e}", align_bytes=DMA_ALIGN)
                 queue = nc.sync if e % 2 == 0 else nc.scalar
                 queue.dma_start(whole[:], w[e])
                 gate_weights.append(whole[:, HALF:M])
@@ -64,6 +65,6 @@ def tile_gather_matmul_kernel(tc, table, w, offs, out):
             for s in range(steps):
                 opened = held.tile([P, blocks, PIECE], F32, name=f"opened{e}_{s}")
                 nc.scalar.activation(opened[:], gates[s][:], SIGMOID)
-                gated = held.tile([P, blocks, PIECE], F32, name=f"gated{e}_{s}")
+                gated = held.tile([P, blocks, PIECE], F32, name=f"gated{e}_{s}", align_bytes=DMA_ALIGN)
                 nc.vector.tensor_tensor(gated[:], values[s][:], opened[:], MULT)
                 nc.sync.dma_start(out_blocks[:, s * blocks : (s + 1) * blocks, e * PIECE : (e + 1) * PIECE], gated[:])

@@ -42,8 +42,7 @@ def tile_gather_matmul_kernel(tc, table, w, offs, out):
                 value_weights.append(value_half[:])
             else:
                 whole = held.tile([P, M], BF16, name=f"whole{e}", align_bytes=DMA_ALIGN)
-                queue = nc.sync if e % 2 == 0 else nc.scalar
-                queue.dma_start(whole[:], w[e])
+                nc.sync.dma_start(whole[:], w[e])
                 gate_weights.append(whole[:, HALF:M])
                 value_weights.append(whole[:, 0:HALF])
 

@@ -12,7 +12,7 @@ M = 512
 HALF = M // 2
 HALF_BLOCKS = 2
 PIECE_COLUMNS = PIECE // 16
-HALVED_EXPERTS = 2
+SCALAR_EXPERTS = 2
 PSUM_BANKS = 8
 DMA_ALIGN = 256
 
@@ -33,18 +33,13 @@ def tile_gather_matmul_kernel(tc, table, w, offs, out):
         gate_weights = []
         value_weights = []
         for e in range(EXPERTS):
-            if e < HALVED_EXPERTS:
-                gate_half = held.tile([P, HALF], BF16, name=f"gate_half{e}", align_bytes=DMA_ALIGN)
-                nc.sync.dma_start(gate_half[:], w[e, :, HALF:M])
-                value_half = held.tile([P, HALF], BF16, name=f"value_half{e}", align_bytes=DMA_ALIGN)
-                nc.scalar.dma_start(value_half[:], w[e, :, 0:HALF])
-                gate_weights.append(gate_half[:])
-                value_weights.append(value_half[:])
-            else:
-                whole = held.tile([P, M], BF16, name=f"whole{e}", align_bytes=DMA_ALIGN)
-                nc.sync.dma_start(whole[:], w[e])
-                gate_weights.append(whole[:, HALF:M])
-                value_weights.append(whole[:, 0:HALF])
+            gate_half = held.tile([P, HALF], BF16, name=f"gate_half{e}", align_bytes=DMA_ALIGN)
+            nc.sync.dma_start(gate_half[:], w[e, :, HALF:M])
+            value_half = held.tile([P, HALF], BF16, name=f"value_half{e}", align_bytes=DMA_ALIGN)
+            value_queue = nc.scalar if e < SCALAR_EXPERTS else nc.sync
+            value_queue.dma_start(value_half[:], w[e, :, 0:HALF])
+            gate_weights.append(gate_half)
+            value_weights.append(value_half)
 
         for e in range(EXPERTS):
             picked = tokens[:].indirect(offsets[:, e * PIECE_COLUMNS : (e + 1) * PIECE_COLUMNS])

@@ -27,7 +27,6 @@ def tile_gather_matmul_kernel(tc, table, w, offs, out):
         tc.psum_pool(name="psum", bufs=PSUM_BANKS) as psum,
     ):
         offsets = held.tile([P, EXPERTS * PIECE_COLUMNS], U16, name="offsets")
-        nc.sync.dma_start(offsets[:], offs)
         tokens = held.tile([P, TOKENS], BF16, name="tokens", align_bytes=DMA_ALIGN)
         nc.scalar.dma_start(tokens[:], table)
         gate_weights = []
@@ -35,6 +34,8 @@ def tile_gather_matmul_kernel(tc, table, w, offs, out):
         for e in range(EXPERTS):
             gate_half = held.tile([P, HALF], BF16, name=f"gate_half{e}", align_bytes=DMA_ALIGN)
             nc.sync.dma_start(gate_half[:], w[e, :, HALF:M])
+            if e == 0:
+                nc.sync.dma_start(offsets[:], offs)
             value_half = held.tile([P, HALF], BF16, name=f"value_half{e}", align_bytes=DMA_ALIGN)
             value_queue = nc.scalar if e < SCALAR_EXPERTS else nc.sync
             value_queue.dma_start(value_half[:], w[e, :, 0:HALF])

import concourse.mybir as mybir

BF16, F32, U16 = mybir.dt.bfloat16, mybir.dt.float32, mybir.dt.uint16
SIGMOID = mybir.ActivationFunctionType.Sigmoid
MULT = mybir.AluOpType.mult

P = 128
TOKENS = 256
EXPERTS = 4
PIECE = 128
M = 512
HALF = M // 2
HALF_BLOCKS = 2
PIECE_COLUMNS = PIECE // 16
SCALAR_EXPERTS = 2
PSUM_BANKS = 8
DMA_ALIGN = 256

FLOPS = 2 * P * M * EXPERTS * PIECE


def tile_gather_matmul_kernel(tc, table, w, offs, out):
    nc = tc.nc
    out_blocks = out.rearrange("(b p) j -> p b j", p=P)
    with (
        tc.tile_pool(name="held", bufs=1) as held,
        tc.psum_pool(name="psum", bufs=PSUM_BANKS) as psum,
    ):
        offsets = held.tile([P, EXPERTS * PIECE_COLUMNS], U16, name="offsets")
        tokens = held.tile([P, TOKENS], BF16, name="tokens", align_bytes=DMA_ALIGN)
        nc.scalar.dma_start(tokens[:], table)
        gate_weights = []
        value_weights = []
        for e in range(EXPERTS):
            gate_half = held.tile([P, HALF], BF16, name=f"gate_half{e}", align_bytes=DMA_ALIGN)
            nc.sync.dma_start(gate_half[:], w[e, :, HALF:M])
            if e == 0:
                nc.sync.dma_start(offsets[:], offs)
            value_half = held.tile([P, HALF], BF16, name=f"value_half{e}", align_bytes=DMA_ALIGN)
            value_queue = nc.scalar if e < SCALAR_EXPERTS else nc.sync
            value_queue.dma_start(value_half[:], w[e, :, 0:HALF])
            gate_weights.append(gate_half)
            value_weights.append(value_half)

        for e in range(EXPERTS):
            picked = tokens[:].indirect(offsets[:, e * PIECE_COLUMNS : (e + 1) * PIECE_COLUMNS])
            steps = HALF_BLOCKS if e == EXPERTS - 1 else 1
            blocks = HALF_BLOCKS // steps
            gates = [psum.tile([P, blocks, PIECE], F32, name=f"gates{e}_{s}", tag="bank") for s in range(steps)]
            values = [psum.tile([P, blocks, PIECE], F32, name=f"values{e}_{s}", tag="bank") for s in range(steps)]
            for b in range(HALF_BLOCKS):
                nc.tensor.matmul(
                    gates[b // blocks][:, b % blocks, :], gate_weights[e][:, b * P : (b + 1) * P], picked, start=True, stop=True
                )
            for b in range(HALF_BLOCKS):
                nc.tensor.matmul(
                    values[b // blocks][:, b % blocks, :], value_weights[e][:, b * P : (b + 1) * P], picked, start=True, stop=True
                )

            for s in range(steps):
                opened = held.tile([P, blocks, PIECE], F32, name=f"opened{e}_{s}")
                nc.scalar.activation(opened[:], gates[s][:], SIGMOID)
                gated = held.tile([P, blocks, PIECE], F32, name=f"gated{e}_{s}", align_bytes=DMA_ALIGN)
                nc.vector.tensor_tensor(gated[:], values[s][:], opened[:], MULT)
                nc.sync.dma_start(out_blocks[:, s * blocks : (s + 1) * blocks, e * PIECE : (e + 1) * PIECE], gated[:])
